import numpy as np
import ml_dtypes


def mxq(x, axis, fmt="e4m3"):
    dtype, down = {"e4m3": (ml_dtypes.float8_e4m3fn, 7), "e5m2": (ml_dtypes.float8_e5m2, 14)}[fmt]
    v = np.moveaxis(np.asarray(x, np.float32).astype(ml_dtypes.bfloat16).astype(np.float64), axis, -1)
    blocks = v.reshape(v.shape[:-1] + (-1, 32))
    amax = np.abs(blocks).max(-1, keepdims=True)
    byte = np.maximum(np.where(amax > 0, np.frexp(amax)[1] - 1 + 127, 0) - down, 1)
    scale = np.exp2(byte - 127.0)
    codes = (blocks / scale).astype(np.float32).astype(dtype).astype(np.float64)
    return np.moveaxis((codes * scale).reshape(v.shape), -1, axis)


WIDE = False


def mx_kscale(k):
    if not WIDE:
        return np.ones(k)
    levels = np.array([10, -10, 5, -5, 0])
    if k % 512:
        return np.exp2(np.random.permutation(np.resize(levels, k // 32))).repeat(32)
    a = np.empty((k // 512, 16))
    for p in range(k // 512):
        a[p, :8] = np.random.permutation(np.resize(levels, 8))
        for g in range(8):
            far = levels[np.abs(levels - a[p, g]) >= 10]
            a[p, g + 8] = far[np.random.randint(len(far))]
    return np.exp2(a.ravel()).repeat(32)


BF16 = ml_dtypes.bfloat16


def bf(x):
    return np.asarray(x, np.float32).astype(BF16)


def f64(x):
    return np.asarray(x).astype(np.float64)


N1, N2, D, T = 6144, 256, 512, 2


def draw0():
    s, t = mx_kscale(D), mx_kscale(D)
    return {"e1": bf(np.random.standard_normal((N1, D)) * s),
            "e2": bf(np.random.standard_normal((N2, D)) / t),
            "w": bf(np.random.standard_normal((T, D, D)) / np.sqrt(D) / s[:, None] * t),
            "v": bf(np.random.standard_normal((T, D)) * 0.5 * t),
            "b": bf(0.3 + 0.1 * np.random.standard_normal(T)),
            "u": bf(np.random.uniform(0.5, 1.5, T))}


def core(e1, e2, w, v, b, u):
    scale = 1.0 / np.sqrt(e1.shape[1])
    t = mxq(f64(e1), 1, "e4m3") @ mxq(f64(w), 1, "e4m3")
    h = t + f64(v)[:, None, :]
    s = scale * (mxq(h, 2, "e4m3") @ mxq(f64(e2), 1, "e4m3").T)
    z = np.tanh(s + f64(b)[:, None, None])
    return np.sum(f64(u)[:, None, None] * z, axis=0)


def e4m3fn_bytes(y):
    return np.clip(np.asarray(y, np.float64), -448.0, 448.0).astype(np.float32).astype(ml_dtypes.float8_e4m3fn).view(np.uint8)


def e4m3fn_values(b):
    return np.asarray(b, np.uint8).view(ml_dtypes.float8_e4m3fn).astype(np.float64)


def setup_inputs():
    d = draw0()
    x0 = np.asarray(d['e1']).astype(np.float64)
    s = (np.max(np.abs(x0), axis=(0,), keepdims=True) / 448.0).astype(np.float32)
    out = {}
    for k, v in d.items():
        if k == 'e1':
            out['e1_bytes'] = e4m3fn_bytes(x0 / s.astype(np.float64))
            out['e1_scale'] = s
        else:
            out[k] = v
    return out


def reference(e1_bytes, e1_scale, e2, w, v, b, u):
    return core(e4m3fn_values(e1_bytes) * e1_scale.astype(np.float64), e2, w, v, b, u)

@@ -1,0 +1,271 @@
+from contextlib import ExitStack
+
+import concourse.mybir as mybir
+from concourse.masks import make_identity
+
+N1, N2, D, T = 6144, 256, 512, 2
+FLOPS = 2 * N1 * D * D * T + 2 * N1 * D * N2 * T
+
+F32 = mybir.dt.float32
+BF16 = mybir.dt.bfloat16
+U32 = mybir.dt.uint32
+U8 = mybir.dt.uint8
+FP8 = mybir.dt.float8_e4m3fn
+FP8X4 = mybir.dt.float8_e4m3fn_x4
+ADD = mybir.AluOpType.add
+MULT = mybir.AluOpType.mult
+ACT = mybir.ActivationFunctionType
+
+P = 128
+PACK = 4
+GROUP = 512
+GROUPS = N1 // GROUP
+STEP = 256
+STEPS = N1 // STEP
+MANUAL = True
+WEIGH = "gpsimd"
+
+
+def tile_pairwiseneuraltensorscorer_t_kernel(tc, e1_bytes, e1_scale, e2, w, v, b, u, out):
+    nc = tc.nc
+    with ExitStack() as ctx:
+        const = ctx.enter_context(tc.tile_pool(name="const", bufs=1))
+        work = ctx.enter_context(tc.tile_pool(name="work", bufs=3))
+        psum = ctx.enter_context(tc.psum_pool(name="psum", bufs=2))
+        single = ctx.enter_context(tc.psum_pool(name="single", bufs=1))
+
+        if MANUAL:
+            ctx.enter_context(tc.manual_schedule())
+
+        e1_rows = e1_bytes.rearrange("(g p j) k -> g p (j k)", p=P, j=4)
+        out_rows = out.rearrange("(g p j) n -> g p j n", p=P, j=4)
+
+        bytes_sb = []
+        for g in range(GROUPS):
+            bytes_tile = const.tile([P, 4 * D], U8, name=f"bytes_sb{g}", align_bytes=64)
+            bytes_sb.append(bytes_tile)
+        scale_sb = const.tile([P, 2, D], F32, name="scale_sb", align_bytes=64)
+        nc.sync.dma_start(out=scale_sb[:, 0, :], in_=e1_scale.rearrange("o k -> (o k)").partition_broadcast(P))
+        nc.sync.dma_start(out=bytes_sb[0][:], in_=e1_rows[0])
+        w_raw = []
+        for s in range(T):
+            w_tile = const.tile([P, PACK, D], BF16, name=f"w_raw{s}", align_bytes=64)
+            nc.sync.dma_start(out=w_tile[:], in_=w[s].rearrange("(p j) c -> p j c", j=PACK))
+            w_raw.append(w_tile)
+        v_sb = const.tile([P, T, PACK], BF16, name="v_sb", align_bytes=64)
+        nc.sync.dma_start(out=v_sb[:], in_=v.rearrange("s (p t) -> p s t", t=PACK))
+        e2_sb = const.tile([P, 2, D], BF16, name="e2_sb", align_bytes=64)
+        nc.sync.dma_start(out=e2_sb[:], in_=e2.rearrange("(r p) k -> p r k", p=P))
+        b_sb = const.tile([P, T], BF16, name="b_sb", align_bytes=64)
+        nc.sync.dma_start(out=b_sb[:], in_=b.partition_broadcast(P))
+        u_sb = const.tile([P, T], BF16, name="u_sb", align_bytes=64)
+        nc.sync.dma_start(out=u_sb[:], in_=u.partition_broadcast(P))
+        for g in range(1, GROUPS):
+            nc.sync.dma_start(out=bytes_sb[g][:], in_=e1_rows[g])
+
+        warm = const.tile([P, 1], F32, name="warm")
+        nc.vector.memset(warm[:], 0.0)
+        warm_out = const.tile([P, 1], F32, name="warm_out")
+        nc.scalar.activation(out=warm_out[:], in_=warm[:], func=ACT.Tanh)
+        ident = const.tile([P, P], F32, name="ident", align_bytes=64)
+        make_identity(nc, ident[:])
+        ident_bf = const.tile([P, P], BF16, name="ident_bf", align_bytes=64)
+        make_identity(nc, ident_bf[:])
+
+        wq, wq_sc = [], []
+        for s in range(T):
+            wq_tile = const.tile([P, D], U32, name=f"wq{s}", align_bytes=64)
+            wq_sc_tile = const.tile([P, D], U8, name=f"wq_sc{s}", align_bytes=64)
+            wq.append(wq_tile)
+            wq_sc.append(wq_sc_tile)
+        e2q = const.tile([P, N2], U32, name="e2q", align_bytes=64)
+        e2q_sc = const.tile([P, N2], U8, name="e2q_sc", align_bytes=64)
+        w_grouped = {}
+
+        def w_interleave(s, engine_copy):
+            grouped = const.tile([P, D, PACK], BF16, name=f"w_grouped{s}", align_bytes=64)
+            w_grouped[s] = grouped
+            engine_copy(
+                out=grouped[:].rearrange("p (t m) j -> p t m j", t=PACK),
+                in_=w_raw[s][:].rearrange("p j (m t) -> p t m j", t=PACK),
+            )
+
+        def w_quantize(s):
+            nc.vector.quantize_mx(out=wq[s][:].bitcast(FP8X4), scales=wq_sc[s][:],
+                                  in_=w_grouped[s][:].rearrange("p c j -> p (c j)"))
+
+        word_bank, xg = {}, {}
+
+        def e2_turn():
+            bank = single.tile([P, 2, STEP], F32, name="words", tag="words")
+            word_bank["e2"] = bank
+            for r in range(2):
+                words = e2_sb[:, r, :].bitcast(F32)
+                for h in range(2):
+                    nc.tensor.transpose(bank[:, h, r * P : (r + 1) * P], words[:, h : 2 * P : 2], ident[:])
+
+        def e2_quantize():
+            nc.vector.quantize_mx(out=e2q[:].bitcast(FP8X4), scales=e2q_sc[:], in_=xg["e2"][:].rearrange("p n j -> p (n j)"))
+
+        x, eq, eq_sc, banks_v, banks_s, hg, planes, hi, hq, hq_sc, sbank, z, zw, woven = ({} for n in range(14))
+
+        def spread_scale():
+            nc.scalar.copy(out=scale_sb[:, 1, :], in_=scale_sb[:, 0, :])
+
+        def prod(i):
+            pieces = 2 if i == 0 else 1
+            x_tile = work.tile([P, 2, D], BF16, name="x", tag="x", align_bytes=64)
+            x[i] = x_tile
+            flat = x_tile[:].rearrange("p j k -> p (j k)")
+            width = 2 * D // pieces
+            for c in range(0, 2 * D, width):
+                col = i % 2 * 2 * D + c
+                nc.vector.tensor_tensor(out=flat[:, c : c + width], in0=bytes_sb[i // 2][:, col : col + width].bitcast(FP8),
+                                        in1=scale_sb[:].rearrange("p j k -> p (j k)")[:, 0:width], op=MULT)
+
+        def turn(i):
+            bank = single.tile([P, 2, STEP], F32, name="words", tag="words")
+            word_bank[i] = bank
+            for j in range(2):
+                words = x[i][:, j, :].bitcast(F32)
+                for h in range(2):
+                    nc.tensor.transpose(bank[:, h, j * P : (j + 1) * P], words[:, h : 2 * P : 2], ident[:])
+
+        def word_exit(i):
+            grouped = work.tile([P, STEP, PACK], BF16, name="e_grouped", tag="e_grouped", align_bytes=64)
+            xg[i] = grouped
+            nc.scalar.copy(out=grouped[:].rearrange("p n j -> p (n j)").bitcast(F32).rearrange("p (n h) -> p n h", h=2),
+                           in_=word_bank[i][:].rearrange("p h n -> p n h"))
+
+        def quantize_e(i):
+            codes = work.tile([P, STEP], U32, name="eq", tag="eq", align_bytes=64)
+            sc = work.tile([P, STEP], U8, name="eq_sc", tag="eq_sc", align_bytes=64)
+            eq[i], eq_sc[i] = codes, sc
+            nc.vector.quantize_mx(out=codes[:].bitcast(FP8X4), scales=sc[:], in_=xg[i][:].rearrange("p n j -> p (n j)"))
+
+        def left_v(i, j):
+            bank = psum.tile([P, PACK, P], F32, name="bank_v", tag="bank_v")
+            banks_v[i, j] = bank
+            cols = slice(j * P, (j + 1) * P)
+            for t in range(PACK):
+                rows = slice(t * P, (t + 1) * P)
+                nc.tensor.matmul_mx(out=bank[:, t, :], lhsT=wq[0][:, rows].bitcast(FP8X4), lhsT_scale=wq_sc[0][:, rows],
+                                    rhs=eq[i][:, cols].bitcast(FP8X4), rhs_scale=eq_sc[i][:, cols], start=True, stop=True)
+
+        def left_s(i, h):
+            bank = psum.tile([P, 2, STEP], F32, name="bank_s", tag="bank_s")
+            banks_s[i, h] = bank
+            for e in range(2):
+                t = 2 * h + e
+                rows = slice(t * P, (t + 1) * P)
+                nc.tensor.matmul_mx(out=bank[:, e, :], lhsT=wq[1][:, rows].bitcast(FP8X4), lhsT_scale=wq_sc[1][:, rows],
+                                    rhs=eq[i][:].bitcast(FP8X4), rhs_scale=eq_sc[i][:], start=True, stop=True)
+
+        def exit_v(i, j):
+            if j == 0:
+                grouped = work.tile([P, STEP, PACK], BF16, name="hg", tag="hg", align_bytes=64)
+                hg[i] = grouped
+            nc.vector.tensor_tensor(out=hg[i][:, j * P : (j + 1) * P, :], in0=banks_v[i, j][:].rearrange("p t n -> p n t"),
+                                    in1=v_sb[:, 0, :].unsqueeze(1).to_broadcast([P, P, PACK]), op=ADD)
+
+        def exit_s(i, h):
+            if h == 0:
+                planes_tile = work.tile([P, PACK, STEP], BF16, name="planes", tag="planes", align_bytes=64)
+                planes[i] = planes_tile
+            for e in range(2):
+                t = 2 * h + e
+                nc.scalar.activation(out=planes[i][:, t, :], in_=banks_s[i, h][:, e, :], func=ACT.Identity,
+                                     bias=v_sb[:, 1, t : t + 1])
+
+        def weave(i):
+            bank = single.tile([P, STEP, PACK], BF16, name="woven", tag="woven")
+            woven[i] = bank
+            for j in range(2):
+                cols = slice(j * P, (j + 1) * P)
+                nc.tensor.matmul(out=bank[:, cols, :].rearrange("p n t -> p (n t)"), lhsT=ident_bf[:],
+                                 rhs=planes[i][:, :, cols].rearrange("p t n -> p n t"), start=True, stop=True)
+
+        def weave_exit(i):
+            grouped = work.tile([P, STEP, PACK], BF16, name="hi", tag="hi", align_bytes=64)
+            hi[i] = grouped
+            nc.scalar.copy(out=grouped[:], in_=woven[i][:])
+
+        def quantize_h(i, s):
+            codes = work.tile([P, STEP], U32, name=f"hq{s}", tag=f"hq{s}", align_bytes=64)
+            sc = work.tile([P, STEP], U8, name=f"hq_sc{s}", tag=f"hq_sc{s}", align_bytes=64)
+            hq[i, s], hq_sc[i, s] = codes, sc
+            src = (hg, hi)[s][i]
+            nc.vector.quantize_mx(out=codes[:].bitcast(FP8X4), scales=sc[:], in_=src[:].rearrange("p n j -> p (n j)"))
+
+        def right(i, s):
+            bank = psum.tile([P, 2, N2], F32, name="sbank", tag="sbank")
+            sbank[i, s] = bank
+            for j in range(2):
+                cols = slice(j * P, (j + 1) * P)
+                nc.tensor.matmul_mx(out=bank[:, j, :], lhsT=hq[i, s][:, cols].bitcast(FP8X4), lhsT_scale=hq_sc[i, s][:, cols],
+                                    rhs=e2q[:].bitcast(FP8X4), rhs_scale=e2q_sc[:], start=True, stop=True)
+
+        def tanh(i, s):
+            z_tile = work.tile([P, 2 * N2], F32, name=f"z{s}", tag=f"z{s}", align_bytes=64)
+            z[i, s] = z_tile
+            nc.scalar.activation(out=z_tile[:], in_=sbank[i, s][:].rearrange("p j n -> p (j n)"), func=ACT.Tanh,
+                                 bias=b_sb[:, s : s + 1], scale=D ** -0.5)
+
+        def weigh(i):
+            if WEIGH == "gpsimd":
+                zw_tile = const.tile([P, 2 * N2], F32, name="zw", tag="zw", align_bytes=64)
+                zw[i] = zw_tile
+                nc.gpsimd.tensor_scalar(out=zw_tile[:], in0=z[i, 0][:], scalar1=u_sb[:, 0:1], scalar2=0.0, op0=MULT, op1=ADD)
+            else:
+                zw_tile = work.tile([P, 2 * N2], F32, name="zw", tag="zw", align_bytes=64)
+                zw[i] = zw_tile
+                nc.vector.tensor_scalar(out=zw_tile[:], in0=z[i, 0][:], scalar1=u_sb[:, 0:1], scalar2=None, op0=MULT)
+
+        def combine(i):
+            o = work.tile([P, 2 * N2], F32, name="o", tag="o", align_bytes=64)
+            nc.vector.scalar_tensor_tensor(out=o[:], in0=z[i, 1][:], scalar=u_sb[:, 1:2], in1=zw[i][:], op0=MULT, op1=ADD)
+            nc.sync.dma_start(out=out_rows[i // 2][:, i % 2 * 2 : i % 2 * 2 + 2, :], in_=o[:].rearrange("p (j n) -> p j n", n=N2))
+
+        def run(f, i, *args):
+            if 0 <= i < STEPS:
+                f(i, *args)
+
+        for i in range(-3, STEPS + 2):
+            if i == -3:
+                spread_scale()
+            run(quantize_h, i - 1, 0)
+            run(left_v, i, 0)
+            run(quantize_h, i - 1, 1)
+            if i == -1:
+                e2_turn()
+            run(prod, i + 3)
+            if i == -1:
+                word_exit("e2")
+            run(tanh, i - 2, 1)
+            run(exit_v, i, 0)
+            if i == -2:
+                w_interleave(1, nc.scalar.copy)
+            run(weigh, i - 2)
+            run(left_s, i + 1, 0)
+            run(exit_s, i + 1, 0)
+            run(right, i - 1, 0)
+            run(tanh, i - 1, 0)
+            run(weave, i)
+            run(left_s, i + 1, 1)
+            run(exit_v, i, 1)
+            run(quantize_e, i + 2)
+            run(right, i - 1, 1)
+            if i == -2:
+                w_quantize(0)
+            run(weave_exit, i)
+            if i == -3:
+                w_interleave(0, nc.vector.tensor_copy)
+            if i == -1:
+                e2_quantize()
+            run(turn, i + 3)
+            run(combine, i - 2)
+            run(exit_s, i + 1, 1)
+            run(left_v, i + 1, 1)
+            if i == -2:
+                w_quantize(1)
+            run(word_exit, i + 3)

@@ -20,10 +20,7 @@ P = 128
 PACK = 4
 GROUP = 512
 GROUPS = N1 // GROUP
-STEP = 256
-STEPS = N1 // STEP
-MANUAL = True
-WEIGH = "gpsimd"
+HALF = 256
 
 
 def tile_pairwiseneuraltensorscorer_t_kernel(tc, e1_bytes, e1_scale, e2, w, v, b, u, out):
@@ -34,8 +31,7 @@ def tile_pairwiseneuraltensorscorer_t_kernel(tc, e1_bytes, e1_scale, e2, w, v, b
         psum = ctx.enter_context(tc.psum_pool(name="psum", bufs=2))
         single = ctx.enter_context(tc.psum_pool(name="single", bufs=1))
 
-        if MANUAL:
-            ctx.enter_context(tc.manual_schedule())
+        ctx.enter_context(tc.manual_schedule())
 
         e1_rows = e1_bytes.rearrange("(g p j) k -> g p (j k)", p=P, j=4)
         out_rows = out.rearrange("(g p j) n -> g p j n", p=P, j=4)
@@ -63,6 +59,7 @@ def tile_pairwiseneuraltensorscorer_t_kernel(tc, e1_bytes, e1_scale, e2, w, v, b
         for g in range(1, GROUPS):
             nc.sync.dma_start(out=bytes_sb[g][:], in_=e1_rows[g])
 
+        u_f32 = const.tile([P, T], F32, name="u_f32", align_bytes=64)
         warm = const.tile([P, 1], F32, name="warm")
         nc.vector.memset(warm[:], 0.0)
         warm_out = const.tile([P, 1], F32, name="warm_out")
@@ -81,6 +78,7 @@ def tile_pairwiseneuraltensorscorer_t_kernel(tc, e1_bytes, e1_scale, e2, w, v, b
         e2q = const.tile([P, N2], U32, name="e2q", align_bytes=64)
         e2q_sc = const.tile([P, N2], U8, name="e2q_sc", align_bytes=64)
         w_grouped = {}
+        e2_grouped = const.tile([P, N2, PACK], BF16, name="e2_grouped", align_bytes=64)
 
         def w_interleave(s, engine_copy):
             grouped = const.tile([P, D, PACK], BF16, name=f"w_grouped{s}", align_bytes=64)
@@ -97,175 +95,192 @@ def tile_pairwiseneuraltensorscorer_t_kernel(tc, e1_bytes, e1_scale, e2, w, v, b
         word_bank, xg = {}, {}
 
         def e2_turn():
-            bank = single.tile([P, 2, STEP], F32, name="words", tag="words")
-            word_bank["e2"] = bank
+            bank = single.tile([P, 2, HALF], F32, name="words", tag="words")
+            word_bank["e2", 0] = bank
             for r in range(2):
                 words = e2_sb[:, r, :].bitcast(F32)
                 for h in range(2):
                     nc.tensor.transpose(bank[:, h, r * P : (r + 1) * P], words[:, h : 2 * P : 2], ident[:])
 
-        def e2_quantize():
-            nc.vector.quantize_mx(out=e2q[:].bitcast(FP8X4), scales=e2q_sc[:], in_=xg["e2"][:].rearrange("p n j -> p (n j)"))
+        def e2_exit():
+            nc.scalar.copy(out=e2_grouped[:].rearrange("p n j -> p (n j)").bitcast(F32).rearrange("p (n h) -> p n h", h=2),
+                           in_=word_bank["e2", 0][:].rearrange("p h n -> p n h"))
 
-        x, eq, eq_sc, banks_v, banks_s, hg, planes, hi, hq, hq_sc, sbank, z, zw, woven = ({} for n in range(14))
+        def e2_quantize():
+            nc.vector.quantize_mx(out=e2q[:].bitcast(FP8X4), scales=e2q_sc[:], in_=e2_grouped[:].rearrange("p n j -> p (n j)"))
+
+        x, eq, eq_sc, banks_v, banks_s, hg, planes, hi, hq, hq_sc, sbank, z, zw, woven, o_sb = ({} for n in range(15))
 
         def spread_scale():
             nc.scalar.copy(out=scale_sb[:, 1, :], in_=scale_sb[:, 0, :])
 
-        def prod(i):
-            pieces = 2 if i == 0 else 1
+        def prod(g, h):
             x_tile = work.tile([P, 2, D], BF16, name="x", tag="x", align_bytes=64)
-            x[i] = x_tile
+            x[g, h] = x_tile
             flat = x_tile[:].rearrange("p j k -> p (j k)")
-            width = 2 * D // pieces
+            width = D if (g, h) == (0, 0) else 2 * D
             for c in range(0, 2 * D, width):
-                col = i % 2 * 2 * D + c
-                nc.vector.tensor_tensor(out=flat[:, c : c + width], in0=bytes_sb[i // 2][:, col : col + width].bitcast(FP8),
+                col = h * 2 * D + c
+                nc.vector.tensor_tensor(out=flat[:, c : c + width], in0=bytes_sb[g][:, col : col + width].bitcast(FP8),
                                         in1=scale_sb[:].rearrange("p j k -> p (j k)")[:, 0:width], op=MULT)
 
-        def turn(i):
-            bank = single.tile([P, 2, STEP], F32, name="words", tag="words")
-            word_bank[i] = bank
+        def turn(g, h):
+            bank = single.tile([P, 2, HALF], F32, name="words", tag="words")
+            word_bank[g, h] = bank
             for j in range(2):
-                words = x[i][:, j, :].bitcast(F32)
-                for h in range(2):
-                    nc.tensor.transpose(bank[:, h, j * P : (j + 1) * P], words[:, h : 2 * P : 2], ident[:])
+                words = x[g, h][:, j, :].bitcast(F32)
+                for e in range(2):
+                    nc.tensor.transpose(bank[:, e, j * P : (j + 1) * P], words[:, e : 2 * P : 2], ident[:])
 
-        def word_exit(i):
-            grouped = work.tile([P, STEP, PACK], BF16, name="e_grouped", tag="e_grouped", align_bytes=64)
-            xg[i] = grouped
-            nc.scalar.copy(out=grouped[:].rearrange("p n j -> p (n j)").bitcast(F32).rearrange("p (n h) -> p n h", h=2),
-                           in_=word_bank[i][:].rearrange("p h n -> p n h"))
+        def word_exit(g, h):
+            if h == 0:
+                grouped = work.tile([P, GROUP, PACK], BF16, name="e_grouped", tag="e_grouped", align_bytes=64)
+                xg[g] = grouped
+            half = xg[g][:, h * HALF : (h + 1) * HALF, :]
+            nc.scalar.copy(out=half.rearrange("p n j -> p (n j)").bitcast(F32).rearrange("p (n e) -> p n e", e=2),
+                           in_=word_bank[g, h][:].rearrange("p e n -> p n e"))
 
-        def quantize_e(i):
-            codes = work.tile([P, STEP], U32, name="eq", tag="eq", align_bytes=64)
-            sc = work.tile([P, STEP], U8, name="eq_sc", tag="eq_sc", align_bytes=64)
-            eq[i], eq_sc[i] = codes, sc
-            nc.vector.quantize_mx(out=codes[:].bitcast(FP8X4), scales=sc[:], in_=xg[i][:].rearrange("p n j -> p (n j)"))
+        def quantize_e(g):
+            codes = work.tile([P, GROUP], U32, name="eq", tag="eq", align_bytes=64)
+            sc = work.tile([P, GROUP], U8, name="eq_sc", tag="eq_sc", align_bytes=64)
+            eq[g], eq_sc[g] = codes, sc
+            nc.vector.quantize_mx(out=codes[:].bitcast(FP8X4), scales=sc[:], in_=xg[g][:].rearrange("p n j -> p (n j)"))
 
-        def left_v(i, j):
+        def left_v(g, j):
             bank = psum.tile([P, PACK, P], F32, name="bank_v", tag="bank_v")
-            banks_v[i, j] = bank
+            banks_v[g, j] = bank
             cols = slice(j * P, (j + 1) * P)
             for t in range(PACK):
                 rows = slice(t * P, (t + 1) * P)
                 nc.tensor.matmul_mx(out=bank[:, t, :], lhsT=wq[0][:, rows].bitcast(FP8X4), lhsT_scale=wq_sc[0][:, rows],
-                                    rhs=eq[i][:, cols].bitcast(FP8X4), rhs_scale=eq_sc[i][:, cols], start=True, stop=True)
+                                    rhs=eq[g][:, cols].bitcast(FP8X4), rhs_scale=eq_sc[g][:, cols], start=True, stop=True)
 
-        def left_s(i, h):
-            bank = psum.tile([P, 2, STEP], F32, name="bank_s", tag="bank_s")
-            banks_s[i, h] = bank
-            for e in range(2):
-                t = 2 * h + e
-                rows = slice(t * P, (t + 1) * P)
-                nc.tensor.matmul_mx(out=bank[:, e, :], lhsT=wq[1][:, rows].bitcast(FP8X4), lhsT_scale=wq_sc[1][:, rows],
-                                    rhs=eq[i][:].bitcast(FP8X4), rhs_scale=eq_sc[i][:], start=True, stop=True)
+        def left_s(g, t):
+            bank = psum.tile([P, GROUP], F32, name="bank_s", tag="bank_s")
+            banks_s[g, t] = bank
+            rows = slice(t * P, (t + 1) * P)
+            nc.tensor.matmul_mx(out=bank[:], lhsT=wq[1][:, rows].bitcast(FP8X4), lhsT_scale=wq_sc[1][:, rows],
+                                rhs=eq[g][:].bitcast(FP8X4), rhs_scale=eq_sc[g][:], start=True, stop=True)
 
-        def exit_v(i, j):
+        def exit_v(g, j):
             if j == 0:
-                grouped = work.tile([P, STEP, PACK], BF16, name="hg", tag="hg", align_bytes=64)
-                hg[i] = grouped
-            nc.vector.tensor_tensor(out=hg[i][:, j * P : (j + 1) * P, :], in0=banks_v[i, j][:].rearrange("p t n -> p n t"),
+                grouped = work.tile([P, GROUP, PACK], BF16, name="hg", tag="hg", align_bytes=64)
+                hg[g] = grouped
+            nc.vector.tensor_tensor(out=hg[g][:, j * P : (j + 1) * P, :], in0=banks_v[g, j][:].rearrange("p t n -> p n t"),
                                     in1=v_sb[:, 0, :].unsqueeze(1).to_broadcast([P, P, PACK]), op=ADD)
 
-        def exit_s(i, h):
-            if h == 0:
-                planes_tile = work.tile([P, PACK, STEP], BF16, name="planes", tag="planes", align_bytes=64)
-                planes[i] = planes_tile
-            for e in range(2):
-                t = 2 * h + e
-                nc.scalar.activation(out=planes[i][:, t, :], in_=banks_s[i, h][:, e, :], func=ACT.Identity,
-                                     bias=v_sb[:, 1, t : t + 1])
+        def exit_s(g, t):
+            if t == 0:
+                planes_tile = work.tile([P, PACK, GROUP], BF16, name="planes", tag="planes", align_bytes=64)
+                planes[g] = planes_tile
+            nc.scalar.activation(out=planes[g][:, t, :], in_=banks_s[g, t][:], func=ACT.Identity, bias=v_sb[:, 1, t : t + 1])
 
-        def weave(i):
-            bank = single.tile([P, STEP, PACK], BF16, name="woven", tag="woven")
-            woven[i] = bank
+        def weave(g, h):
+            bank = single.tile([P, HALF, PACK], BF16, name="woven", tag="woven")
+            woven[g, h] = bank
             for j in range(2):
-                cols = slice(j * P, (j + 1) * P)
-                nc.tensor.matmul(out=bank[:, cols, :].rearrange("p n t -> p (n t)"), lhsT=ident_bf[:],
-                                 rhs=planes[i][:, :, cols].rearrange("p t n -> p n t"), start=True, stop=True)
+                cols = slice((2 * h + j) * P, (2 * h + j + 1) * P)
+                nc.tensor.matmul(out=bank[:, j * P : (j + 1) * P, :].rearrange("p n t -> p (n t)"), lhsT=ident_bf[:],
+                                 rhs=planes[g][:, :, cols].rearrange("p t n -> p n t"), start=True, stop=True)
 
-        def weave_exit(i):
-            grouped = work.tile([P, STEP, PACK], BF16, name="hi", tag="hi", align_bytes=64)
-            hi[i] = grouped
-            nc.scalar.copy(out=grouped[:], in_=woven[i][:])
+        def weave_exit(g, h):
+            if h == 0:
+                grouped = work.tile([P, GROUP, PACK], BF16, name="hi", tag="hi", align_bytes=64)
+                hi[g] = grouped
+            nc.scalar.copy(out=hi[g][:, h * HALF : (h + 1) * HALF, :], in_=woven[g, h][:])
 
-        def quantize_h(i, s):
-            codes = work.tile([P, STEP], U32, name=f"hq{s}", tag=f"hq{s}", align_bytes=64)
-            sc = work.tile([P, STEP], U8, name=f"hq_sc{s}", tag=f"hq_sc{s}", align_bytes=64)
-            hq[i, s], hq_sc[i, s] = codes, sc
-            src = (hg, hi)[s][i]
+        def quantize_h(g, s):
+            codes = work.tile([P, GROUP], U32, name=f"hq{s}", tag=f"hq{s}", align_bytes=64)
+            sc = work.tile([P, GROUP], U8, name=f"hq_sc{s}", tag=f"hq_sc{s}", align_bytes=64)
+            hq[g, s], hq_sc[g, s] = codes, sc
+            src = (hg, hi)[s][g]
             nc.vector.quantize_mx(out=codes[:].bitcast(FP8X4), scales=sc[:], in_=src[:].rearrange("p n j -> p (n j)"))
 
-        def right(i, s):
+        def right(g, s, h):
             bank = psum.tile([P, 2, N2], F32, name="sbank", tag="sbank")
-            sbank[i, s] = bank
+            sbank[g, s, h] = bank
             for j in range(2):
-                cols = slice(j * P, (j + 1) * P)
-                nc.tensor.matmul_mx(out=bank[:, j, :], lhsT=hq[i, s][:, cols].bitcast(FP8X4), lhsT_scale=hq_sc[i, s][:, cols],
+                cols = slice((2 * h + j) * P, (2 * h + j + 1) * P)
+                nc.tensor.matmul_mx(out=bank[:, j, :], lhsT=hq[g, s][:, cols].bitcast(FP8X4), lhsT_scale=hq_sc[g, s][:, cols],
                                     rhs=e2q[:].bitcast(FP8X4), rhs_scale=e2q_sc[:], start=True, stop=True)
 
-        def tanh(i, s):
-            z_tile = work.tile([P, 2 * N2], F32, name=f"z{s}", tag=f"z{s}", align_bytes=64)
-            z[i, s] = z_tile
-            nc.scalar.activation(out=z_tile[:], in_=sbank[i, s][:].rearrange("p j n -> p (j n)"), func=ACT.Tanh,
+        def tanh(g, s, h):
+            z_tile = work.tile([P, 2 * N2], F32, name=f"z{s}{h}", tag=f"z{s}{h}", align_bytes=64)
+            z[g, s, h] = z_tile
+            nc.scalar.activation(out=z_tile[:], in_=sbank[g, s, h][:].rearrange("p j n -> p (j n)"), func=ACT.Tanh,
                                  bias=b_sb[:, s : s + 1], scale=D ** -0.5)
 
-        def weigh(i):
-            if WEIGH == "gpsimd":
-                zw_tile = const.tile([P, 2 * N2], F32, name="zw", tag="zw", align_bytes=64)
-                zw[i] = zw_tile
-                nc.gpsimd.tensor_scalar(out=zw_tile[:], in0=z[i, 0][:], scalar1=u_sb[:, 0:1], scalar2=0.0, op0=MULT, op1=ADD)
-            else:
-                zw_tile = work.tile([P, 2 * N2], F32, name="zw", tag="zw", align_bytes=64)
-                zw[i] = zw_tile
-                nc.vector.tensor_scalar(out=zw_tile[:], in0=z[i, 0][:], scalar1=u_sb[:, 0:1], scalar2=None, op0=MULT)
+        def weigh(g, h):
+            zw_tile = const.tile([P, 2 * N2], F32, name=f"zw{h}", tag=f"zw{h}", align_bytes=64)
+            zw[g, h] = zw_tile
+            nc.gpsimd.tensor_scalar(out=zw_tile[:], in0=z[g, 0, h][:], scalar1=u_f32[:, 0:1], scalar2=0.0, op0=MULT, op1=ADD)
 
-        def combine(i):
-            o = work.tile([P, 2 * N2], F32, name="o", tag="o", align_bytes=64)
-            nc.vector.scalar_tensor_tensor(out=o[:], in0=z[i, 1][:], scalar=u_sb[:, 1:2], in1=zw[i][:], op0=MULT, op1=ADD)
-            nc.sync.dma_start(out=out_rows[i // 2][:, i % 2 * 2 : i % 2 * 2 + 2, :], in_=o[:].rearrange("p (j n) -> p j n", n=N2))
+        def combine(g, h):
+            o = work.tile([P, 2 * N2], F32, name=f"o{h}", tag=f"o{h}", align_bytes=64)
+            nc.vector.scalar_tensor_tensor(out=o[:], in0=z[g, 1, h][:], scalar=u_f32[:, 1:2], in1=zw[g, h][:], op0=MULT, op1=ADD)
+            nc.sync.dma_start(out=out_rows[g][:, 2 * h : 2 * h + 2, :], in_=o[:].rearrange("p (j n) -> p j n", n=N2))
 
-        def run(f, i, *args):
-            if 0 <= i < STEPS:
-                f(i, *args)
+        def run(f, g, *args):
+            if 0 <= g < GROUPS:
+                f(g, *args)
 
-        for i in range(-3, STEPS + 2):
-            if i == -3:
+        for i in range(-4, GROUPS + 2):
+            run(turn, i + 1, 1)
+            if i == -4:
                 spread_scale()
-            run(quantize_h, i - 1, 0)
-            run(left_v, i, 0)
-            run(quantize_h, i - 1, 1)
+            run(right, i - 1, 0, 1)
+            run(tanh, i - 2, 1, 0)
+            run(exit_s, i, 3)
             if i == -1:
-                e2_turn()
-            run(prod, i + 3)
-            if i == -1:
-                word_exit("e2")
-            run(tanh, i - 2, 1)
-            run(exit_v, i, 0)
-            if i == -2:
-                w_interleave(1, nc.scalar.copy)
-            run(weigh, i - 2)
-            run(left_s, i + 1, 0)
-            run(exit_s, i + 1, 0)
-            run(right, i - 1, 0)
-            run(tanh, i - 1, 0)
-            run(weave, i)
-            run(left_s, i + 1, 1)
+                w_quantize(1)
             run(exit_v, i, 1)
-            run(quantize_e, i + 2)
-            run(right, i - 1, 1)
-            if i == -2:
-                w_quantize(0)
-            run(weave_exit, i)
+            run(weave_exit, i - 1, 1)
+            run(weigh, i - 2, 0)
+            run(exit_s, i, 1)
+            run(left_s, i, 2)
+            run(right, i - 1, 0, 0)
+            run(quantize_h, i - 1, 1)
+            run(left_v, i, 2)
+            run(word_exit, i + 1, 1)
             if i == -3:
-                w_interleave(0, nc.vector.tensor_copy)
+                w_quantize(0)
+            run(exit_s, i, 2)
             if i == -1:
                 e2_quantize()
-            run(turn, i + 3)
-            run(combine, i - 2)
-            run(exit_s, i + 1, 1)
-            run(left_v, i + 1, 1)
+            run(tanh, i - 1, 0, 1)
             if i == -2:
-                w_quantize(1)
-            run(word_exit, i + 3)
+                w_interleave(1, nc.scalar.copy)
+            run(combine, i - 2, 1)
+            run(tanh, i - 1, 0, 0)
+            run(left_v, i, 3)
+            run(turn, i + 2, 0)
+            run(word_exit, i + 2, 0)
+            run(weave, i, 0)
+            run(quantize_e, i + 1)
+            run(weave_exit, i, 0)
+            run(right, i - 1, 1, 1)
+            run(left_s, i + 1, 0)
+            run(exit_v, i, 2)
+            run(exit_v, i, 3)
+            run(prod, i + 2, 1)
+            run(right, i - 1, 1, 0)
+            run(left_s, i + 1, 3)
+            if i == -2:
+                e2_turn()
+            run(left_v, i + 1, 0)
+            run(tanh, i - 1, 1, 1)
+            run(weave, i, 1)
+            run(quantize_h, i, 0)
+            if i == -2:
+                e2_exit()
+            run(left_v, i + 1, 1)
+            run(exit_s, i + 1, 0)
+            run(weigh, i - 1, 1)
+            if i == 0:
+                nc.gpsimd.tensor_copy(out=u_f32[:], in_=u_sb[:])
+            run(combine, i - 2, 0)
+            run(prod, i + 4, 0)
+            run(exit_v, i + 1, 0)
+            if i == -4:
+                w_interleave(0, nc.vector.tensor_copy)
+            run(left_s, i + 1, 1)

@@ -211,9 +211,12 @@ def tile_pairwiseneuraltensorscorer_t_kernel(tc, e1_bytes, e1_scale, e2, w, v, b
                                  bias=b_sb[:, s : s + 1], scale=D ** -0.5)
 
         def weigh(g, h):
-            zw_tile = const.tile([P, 2 * N2], F32, name=f"zw{h}", tag=f"zw{h}", align_bytes=64)
+            zw_tile = work.tile([P, 2 * N2], F32, name=f"zw{h}", tag=f"zw{h}", align_bytes=64)
             zw[g, h] = zw_tile
-            nc.gpsimd.tensor_scalar(out=zw_tile[:], in0=z[g, 0, h][:], scalar1=u_f32[:, 0:1], scalar2=0.0, op0=MULT, op1=ADD)
+            if h == 0:
+                nc.vector.tensor_scalar(out=zw_tile[:], in0=z[g, 0, h][:], scalar1=u_f32[:, 0:1], scalar2=None, op0=MULT)
+            else:
+                nc.scalar.activation(out=zw_tile[:], in_=z[g, 0, h][:], func=ACT.Copy, scale=u_f32[:, 0:1])
 
         def combine(g, h):
             o = work.tile([P, 2 * N2], F32, name=f"o{h}", tag=f"o{h}", align_bytes=64)
@@ -224,63 +227,63 @@ def tile_pairwiseneuraltensorscorer_t_kernel(tc, e1_bytes, e1_scale, e2, w, v, b
             if 0 <= g < GROUPS:
                 f(g, *args)
 
-        for i in range(-4, GROUPS + 2):
-            run(turn, i + 1, 1)
-            if i == -4:
-                spread_scale()
-            run(right, i - 1, 0, 1)
+        for i in range(-3, GROUPS + 4):
             run(tanh, i - 2, 1, 0)
-            run(exit_s, i, 3)
+            run(exit_v, i - 1, 3)
+            run(left_v, i, 0)
+            run(weigh, i - 3, 0)
+            run(exit_v, i - 1, 2)
+            if i == -2:
+                spread_scale()
+            run(left_v, i, 1)
+            run(weave, i - 1, 1)
+            if i == -1:
+                w_interleave(1, nc.scalar.copy)
+            run(exit_s, i, 0)
+            run(prod, i + 2, 1)
+            run(quantize_h, i - 1, 0)
             if i == -1:
                 w_quantize(1)
-            run(exit_v, i, 1)
-            run(weave_exit, i - 1, 1)
-            run(weigh, i - 2, 0)
-            run(exit_s, i, 1)
-            run(left_s, i, 2)
-            run(right, i - 1, 0, 0)
-            run(quantize_h, i - 1, 1)
-            run(left_v, i, 2)
-            run(word_exit, i + 1, 1)
-            if i == -3:
-                w_quantize(0)
-            run(exit_s, i, 2)
+            run(exit_v, i, 0)
+            run(tanh, i - 2, 1, 1)
             if i == -1:
-                e2_quantize()
-            run(tanh, i - 1, 0, 1)
-            if i == -2:
-                w_interleave(1, nc.scalar.copy)
-            run(combine, i - 2, 1)
-            run(tanh, i - 1, 0, 0)
-            run(left_v, i, 3)
-            run(turn, i + 2, 0)
-            run(word_exit, i + 2, 0)
-            run(weave, i, 0)
-            run(quantize_e, i + 1)
-            run(weave_exit, i, 0)
-            run(right, i - 1, 1, 1)
-            run(left_s, i + 1, 0)
-            run(exit_v, i, 2)
-            run(exit_v, i, 3)
-            run(prod, i + 2, 1)
-            run(right, i - 1, 1, 0)
-            run(left_s, i + 1, 3)
-            if i == -2:
                 e2_turn()
-            run(left_v, i + 1, 0)
-            run(tanh, i - 1, 1, 1)
-            run(weave, i, 1)
-            run(quantize_h, i, 0)
+            run(combine, i - 4, 1)
+            run(exit_v, i, 1)
+            run(exit_s, i, 3)
             if i == -2:
-                e2_exit()
-            run(left_v, i + 1, 1)
-            run(exit_s, i + 1, 0)
-            run(weigh, i - 1, 1)
-            if i == 0:
                 nc.gpsimd.tensor_copy(out=u_f32[:], in_=u_sb[:])
-            run(combine, i - 2, 0)
-            run(prod, i + 4, 0)
-            run(exit_v, i + 1, 0)
-            if i == -4:
+            run(left_s, i, 1)
+            run(combine, i - 3, 0)
+            if i == -1:
+                e2_exit()
+            run(weave_exit, i - 1, 1)
+            run(turn, i + 1, 1)
+            run(prod, i + 3, 0)
+            run(quantize_h, i - 1, 1)
+            if i == -3:
                 w_interleave(0, nc.vector.tensor_copy)
-            run(left_s, i + 1, 1)
+            run(left_s, i, 2)
+            run(right, i - 1, 0, 1)
+            run(left_v, i, 3)
+            run(exit_s, i, 1)
+            run(left_v, i, 2)
+            run(right, i - 1, 0, 0)
+            run(word_exit, i + 1, 1)
+            run(exit_s, i, 2)
+            if i == 0:
+                e2_quantize()
+            run(turn, i + 2, 0)
+            run(quantize_e, i + 1)
+            run(tanh, i - 1, 0, 1)
+            if i == -1:
+                w_quantize(0)
+            run(tanh, i - 1, 0, 0)
+            run(weave, i, 0)
+            run(right, i - 1, 1, 0)
+            run(right, i - 1, 1, 1)
+            run(word_exit, i + 2, 0)
+            run(left_s, i + 1, 0)
+            run(left_s, i + 1, 3)
+            run(weigh, i - 2, 1)
+            run(weave_exit, i, 0)

@@ -29,7 +29,7 @@ def tile_pairwiseneuraltensorscorer_t_kernel(tc, e1_bytes, e1_scale, e2, w, v, b
         const = ctx.enter_context(tc.tile_pool(name="const", bufs=1))
         work = ctx.enter_context(tc.tile_pool(name="work", bufs=3))
         psum = ctx.enter_context(tc.psum_pool(name="psum", bufs=2))
-        single = ctx.enter_context(tc.psum_pool(name="single", bufs=1))
+        single = ctx.enter_context(tc.psum_pool(name="single", bufs=2))
 
         ctx.enter_context(tc.manual_schedule())
 
@@ -95,7 +95,7 @@ def tile_pairwiseneuraltensorscorer_t_kernel(tc, e1_bytes, e1_scale, e2, w, v, b
         word_bank, xg = {}, {}
 
         def e2_turn():
-            bank = single.tile([P, 2, HALF], F32, name="words", tag="words")
+            bank = single.tile([P, 2, HALF], F32, name="words", tag="flex")
             word_bank["e2", 0] = bank
             for r in range(2):
                 words = e2_sb[:, r, :].bitcast(F32)
@@ -125,7 +125,7 @@ def tile_pairwiseneuraltensorscorer_t_kernel(tc, e1_bytes, e1_scale, e2, w, v, b
                                         in1=scale_sb[:].rearrange("p j k -> p (j k)")[:, 0:width], op=MULT)
 
         def turn(g, h):
-            bank = single.tile([P, 2, HALF], F32, name="words", tag="words")
+            bank = single.tile([P, 2, HALF], F32, name="words", tag="flex")
             word_bank[g, h] = bank
             for j in range(2):
                 words = x[g, h][:, j, :].bitcast(F32)
@@ -176,18 +176,25 @@ def tile_pairwiseneuraltensorscorer_t_kernel(tc, e1_bytes, e1_scale, e2, w, v, b
             nc.scalar.activation(out=planes[g][:, t, :], in_=banks_s[g, t][:], func=ACT.Identity, bias=v_sb[:, 1, t : t + 1])
 
         def weave(g, h):
-            bank = single.tile([P, HALF, PACK], BF16, name="woven", tag="woven")
+            if h == 1 and g % 2 == 1:
+                return
+            bank = single.tile([P, HALF, PACK], BF16, name="woven", tag="flex")
             woven[g, h] = bank
             for j in range(2):
                 cols = slice((2 * h + j) * P, (2 * h + j + 1) * P)
-                nc.tensor.matmul(out=bank[:, j * P : (j + 1) * P, :].rearrange("p n t -> p (n t)"), lhsT=ident_bf[:],
-                                 rhs=planes[g][:, :, cols].rearrange("p t n -> p n t"), start=True, stop=True)
+                nc.tensor.matmul(out=bank[:, j * P : (j + 1) * P, :].rearrange("p n t -> p t n"), lhsT=ident_bf[:],
+                                 rhs=planes[g][:, :, cols], start=True, stop=True)
 
         def weave_exit(g, h):
             if h == 0:
                 grouped = work.tile([P, GROUP, PACK], BF16, name="hi", tag="hi", align_bytes=64)
                 hi[g] = grouped
-            nc.scalar.copy(out=hi[g][:, h * HALF : (h + 1) * HALF, :], in_=woven[g, h][:])
+            cols = slice(h * HALF, (h + 1) * HALF)
+            if (g, h) in woven:
+                nc.scalar.copy(out=hi[g][:, cols, :], in_=woven[g, h][:])
+            else:
+                nc.scalar.copy(out=hi[g][:, cols, :].rearrange("p (c i) t -> p c t i", i=4),
+                               in_=planes[g][:, :, cols].rearrange("p t (c i) -> p c t i", i=4))
 
         def quantize_h(g, s):
             codes = work.tile([P, GROUP], U32, name=f"hq{s}", tag=f"hq{s}", align_bytes=64)
@@ -211,12 +218,9 @@ def tile_pairwiseneuraltensorscorer_t_kernel(tc, e1_bytes, e1_scale, e2, w, v, b
                                  bias=b_sb[:, s : s + 1], scale=D ** -0.5)
 
         def weigh(g, h):
-            zw_tile = work.tile([P, 2 * N2], F32, name=f"zw{h}", tag=f"zw{h}", align_bytes=64)
+            zw_tile = const.tile([P, 2 * N2], F32, name=f"zw{h}", tag=f"zw{h}", align_bytes=64)
             zw[g, h] = zw_tile
-            if h == 0:
-                nc.vector.tensor_scalar(out=zw_tile[:], in0=z[g, 0, h][:], scalar1=u_f32[:, 0:1], scalar2=None, op0=MULT)
-            else:
-                nc.scalar.activation(out=zw_tile[:], in_=z[g, 0, h][:], func=ACT.Copy, scale=u_f32[:, 0:1])
+            nc.gpsimd.tensor_scalar(out=zw_tile[:], in0=z[g, 0, h][:], scalar1=u_f32[:, 0:1], scalar2=0.0, op0=MULT, op1=ADD)
 
         def combine(g, h):
             o = work.tile([P, 2 * N2], F32, name=f"o{h}", tag=f"o{h}", align_bytes=64)
@@ -227,63 +231,63 @@ def tile_pairwiseneuraltensorscorer_t_kernel(tc, e1_bytes, e1_scale, e2, w, v, b
             if 0 <= g < GROUPS:
                 f(g, *args)
 
-        for i in range(-3, GROUPS + 4):
-            run(tanh, i - 2, 1, 0)
-            run(exit_v, i - 1, 3)
-            run(left_v, i, 0)
-            run(weigh, i - 3, 0)
-            run(exit_v, i - 1, 2)
-            if i == -2:
-                spread_scale()
-            run(left_v, i, 1)
-            run(weave, i - 1, 1)
-            if i == -1:
-                w_interleave(1, nc.scalar.copy)
-            run(exit_s, i, 0)
-            run(prod, i + 2, 1)
-            run(quantize_h, i - 1, 0)
-            if i == -1:
-                w_quantize(1)
-            run(exit_v, i, 0)
-            run(tanh, i - 2, 1, 1)
+        for i in range(-3, GROUPS + 3):
+            run(weigh, i - 2, 1)
             if i == -1:
                 e2_turn()
-            run(combine, i - 4, 1)
-            run(exit_v, i, 1)
-            run(exit_s, i, 3)
-            if i == -2:
-                nc.gpsimd.tensor_copy(out=u_f32[:], in_=u_sb[:])
+            if i == -3:
+                spread_scale()
+            if i == 1:
+                e2_quantize()
+            run(word_exit, i + 1, 1)
+            run(quantize_e, i + 1)
+            run(left_v, i, 0)
+            run(tanh, i - 2, 0, 0)
             run(left_s, i, 1)
+            run(exit_s, i, 2)
+            run(weave, i - 1, 1)
             run(combine, i - 3, 0)
+            run(tanh, i - 2, 1, 1)
+            run(left_v, i, 1)
+            run(exit_s, i, 1)
+            if i == -2:
+                w_interleave(0, nc.vector.tensor_copy)
+            run(quantize_h, i - 1, 0)
+            run(turn, i + 2, 0)
             if i == -1:
                 e2_exit()
             run(weave_exit, i - 1, 1)
-            run(turn, i + 1, 1)
-            run(prod, i + 3, 0)
-            run(quantize_h, i - 1, 1)
-            if i == -3:
-                w_interleave(0, nc.vector.tensor_copy)
-            run(left_s, i, 2)
-            run(right, i - 1, 0, 1)
-            run(left_v, i, 3)
-            run(exit_s, i, 1)
-            run(left_v, i, 2)
-            run(right, i - 1, 0, 0)
-            run(word_exit, i + 1, 1)
-            run(exit_s, i, 2)
-            if i == 0:
-                e2_quantize()
-            run(turn, i + 2, 0)
-            run(quantize_e, i + 1)
-            run(tanh, i - 1, 0, 1)
+            run(exit_v, i, 0)
+            run(right, i - 2, 1, 0)
+            run(left_s, i + 1, 0)
+            if i == -2:
+                w_interleave(1, nc.scalar.copy)
+            run(left_s, i + 1, 3)
+            run(exit_v, i, 1)
+            run(word_exit, i + 2, 0)
+            run(prod, i + 3, 1)
             if i == -1:
                 w_quantize(0)
-            run(tanh, i - 1, 0, 0)
+            run(right, i - 1, 0, 1)
+            run(tanh, i - 2, 1, 0)
+            run(exit_s, i + 1, 0)
+            run(combine, i - 2, 1)
+            run(left_v, i, 3)
+            run(tanh, i - 1, 0, 1)
+            run(exit_s, i + 1, 3)
             run(weave, i, 0)
-            run(right, i - 1, 1, 0)
-            run(right, i - 1, 1, 1)
-            run(word_exit, i + 2, 0)
-            run(left_s, i + 1, 0)
-            run(left_s, i + 1, 3)
-            run(weigh, i - 2, 1)
             run(weave_exit, i, 0)
+            run(turn, i + 2, 1)
+            run(quantize_h, i - 1, 1)
+            run(right, i - 1, 0, 0)
+            run(left_v, i, 2)
+            run(exit_v, i, 3)
+            if i == 0:
+                nc.gpsimd.tensor_copy(out=u_f32[:], in_=u_sb[:])
+            run(prod, i + 3, 0)
+            run(left_s, i + 1, 2)
+            run(weigh, i - 2, 0)
+            if i == -2:
+                w_quantize(1)
+            run(exit_v, i, 2)
+            run(right, i - 1, 1, 1)

from contextlib import ExitStack

import concourse.mybir as mybir
from concourse.masks import make_identity

N1, N2, D, T = 6144, 256, 512, 2
FLOPS = 2 * N1 * D * D * T + 2 * N1 * D * N2 * T

F32 = mybir.dt.float32
BF16 = mybir.dt.bfloat16
U32 = mybir.dt.uint32
U8 = mybir.dt.uint8
FP8 = mybir.dt.float8_e4m3fn
FP8X4 = mybir.dt.float8_e4m3fn_x4
ADD = mybir.AluOpType.add
MULT = mybir.AluOpType.mult
ACT = mybir.ActivationFunctionType

P = 128
PACK = 4
GROUP = 512
GROUPS = N1 // GROUP
HALF = 256


def tile_pairwiseneuraltensorscorer_t_kernel(tc, e1_bytes, e1_scale, e2, w, v, b, u, out):
    nc = tc.nc
    with ExitStack() as ctx:
        const = ctx.enter_context(tc.tile_pool(name="const", bufs=1))
        work = ctx.enter_context(tc.tile_pool(name="work", bufs=3))
        psum = ctx.enter_context(tc.psum_pool(name="psum", bufs=2))
        single = ctx.enter_context(tc.psum_pool(name="single", bufs=2))

        ctx.enter_context(tc.manual_schedule())

        e1_rows = e1_bytes.rearrange("(g p j) k -> g p (j k)", p=P, j=4)
        out_rows = out.rearrange("(g p j) n -> g p j n", p=P, j=4)

        bytes_sb = []
        for g in range(GROUPS):
            bytes_tile = const.tile([P, 4 * D], U8, name=f"bytes_sb{g}", align_bytes=64)
            bytes_sb.append(bytes_tile)
        scale_sb = const.tile([P, 2, D], F32, name="scale_sb", align_bytes=64)
        nc.sync.dma_start(out=scale_sb[:, 0, :], in_=e1_scale.rearrange("o k -> (o k)").partition_broadcast(P))
        nc.sync.dma_start(out=bytes_sb[0][:], in_=e1_rows[0])
        w_raw = []
        for s in range(T):
            w_tile = const.tile([P, PACK, D], BF16, name=f"w_raw{s}", align_bytes=64)
            nc.sync.dma_start(out=w_tile[:], in_=w[s].rearrange("(p j) c -> p j c", j=PACK))
            w_raw.append(w_tile)
        v_sb = const.tile([P, T, PACK], BF16, name="v_sb", align_bytes=64)
        nc.sync.dma_start(out=v_sb[:], in_=v.rearrange("s (p t) -> p s t", t=PACK))
        e2_sb = const.tile([P, 2, D], BF16, name="e2_sb", align_bytes=64)
        nc.sync.dma_start(out=e2_sb[:], in_=e2.rearrange("(r p) k -> p r k", p=P))
        b_sb = const.tile([P, T], BF16, name="b_sb", align_bytes=64)
        nc.sync.dma_start(out=b_sb[:], in_=b.partition_broadcast(P))
        u_sb = const.tile([P, T], BF16, name="u_sb", align_bytes=64)
        nc.sync.dma_start(out=u_sb[:], in_=u.partition_broadcast(P))
        for g in range(1, GROUPS):
            nc.sync.dma_start(out=bytes_sb[g][:], in_=e1_rows[g])

        u_f32 = const.tile([P, T], F32, name="u_f32", align_bytes=64)
        warm = const.tile([P, 1], F32, name="warm")
        nc.vector.memset(warm[:], 0.0)
        warm_out = const.tile([P, 1], F32, name="warm_out")
        nc.scalar.activation(out=warm_out[:], in_=warm[:], func=ACT.Tanh)
        ident = const.tile([P, P], F32, name="ident", align_bytes=64)
        make_identity(nc, ident[:])
        ident_bf = const.tile([P, P], BF16, name="ident_bf", align_bytes=64)
        make_identity(nc, ident_bf[:])

        wq, wq_sc = [], []
        for s in range(T):
            wq_tile = const.tile([P, D], U32, name=f"wq{s}", align_bytes=64)
            wq_sc_tile = const.tile([P, D], U8, name=f"wq_sc{s}", align_bytes=64)
            wq.append(wq_tile)
            wq_sc.append(wq_sc_tile)
        e2q = const.tile([P, N2], U32, name="e2q", align_bytes=64)
        e2q_sc = const.tile([P, N2], U8, name="e2q_sc", align_bytes=64)
        w_grouped = {}
        e2_grouped = const.tile([P, N2, PACK], BF16, name="e2_grouped", align_bytes=64)

        def w_interleave(s, engine_copy):
            grouped = const.tile([P, D, PACK], BF16, name=f"w_grouped{s}", align_bytes=64)
            w_grouped[s] = grouped
            engine_copy(
                out=grouped[:].rearrange("p (t m) j -> p t m j", t=PACK),
                in_=w_raw[s][:].rearrange("p j (m t) -> p t m j", t=PACK),
            )

        def w_quantize(s):
            nc.vector.quantize_mx(out=wq[s][:].bitcast(FP8X4), scales=wq_sc[s][:],
                                  in_=w_grouped[s][:].rearrange("p c j -> p (c j)"))

        word_bank, xg = {}, {}

        def e2_turn():
            bank = single.tile([P, 2, HALF], F32, name="words", tag="flex")
            word_bank["e2", 0] = bank
            for r in range(2):
                words = e2_sb[:, r, :].bitcast(F32)
                for h in range(2):
                    nc.tensor.transpose(bank[:, h, r * P : (r + 1) * P], words[:, h : 2 * P : 2], ident[:])

        def e2_exit():
            nc.scalar.copy(out=e2_grouped[:].rearrange("p n j -> p (n j)").bitcast(F32).rearrange("p (n h) -> p n h", h=2),
                           in_=word_bank["e2", 0][:].rearrange("p h n -> p n h"))

        def e2_quantize():
            nc.vector.quantize_mx(out=e2q[:].bitcast(FP8X4), scales=e2q_sc[:], in_=e2_grouped[:].rearrange("p n j -> p (n j)"))

        x, eq, eq_sc, banks_v, banks_s, hg, planes, hi, hq, hq_sc, sbank, z, zw, woven, o_sb = ({} for n in range(15))

        def spread_scale():
            nc.scalar.copy(out=scale_sb[:, 1, :], in_=scale_sb[:, 0, :])

        def prod(g, h):
            x_tile = work.tile([P, 2, D], BF16, name="x", tag="x", align_bytes=64)
            x[g, h] = x_tile
            flat = x_tile[:].rearrange("p j k -> p (j k)")
            width = D if (g, h) == (0, 0) else 2 * D
            for c in range(0, 2 * D, width):
                col = h * 2 * D + c
                nc.vector.tensor_tensor(out=flat[:, c : c + width], in0=bytes_sb[g][:, col : col + width].bitcast(FP8),
                                        in1=scale_sb[:].rearrange("p j k -> p (j k)")[:, 0:width], op=MULT)

        def turn(g, h):
            bank = single.tile([P, 2, HALF], F32, name="words", tag="flex")
            word_bank[g, h] = bank
            for j in range(2):
                words = x[g, h][:, j, :].bitcast(F32)
                for e in range(2):
                    nc.tensor.transpose(bank[:, e, j * P : (j + 1) * P], words[:, e : 2 * P : 2], ident[:])

        def word_exit(g, h):
            if h == 0:
                grouped = work.tile([P, GROUP, PACK], BF16, name="e_grouped", tag="e_grouped", align_bytes=64)
                xg[g] = grouped
            half = xg[g][:, h * HALF : (h + 1) * HALF, :]
            nc.scalar.copy(out=half.rearrange("p n j -> p (n j)").bitcast(F32).rearrange("p (n e) -> p n e", e=2),
                           in_=word_bank[g, h][:].rearrange("p e n -> p n e"))

        def quantize_e(g):
            codes = work.tile([P, GROUP], U32, name="eq", tag="eq", align_bytes=64)
            sc = work.tile([P, GROUP], U8, name="eq_sc", tag="eq_sc", align_bytes=64)
            eq[g], eq_sc[g] = codes, sc
            nc.vector.quantize_mx(out=codes[:].bitcast(FP8X4), scales=sc[:], in_=xg[g][:].rearrange("p n j -> p (n j)"))

        def left_v(g, j):
            bank = psum.tile([P, PACK, P], F32, name="bank_v", tag="bank_v")
            banks_v[g, j] = bank
            cols = slice(j * P, (j + 1) * P)
            for t in range(PACK):
                rows = slice(t * P, (t + 1) * P)
                nc.tensor.matmul_mx(out=bank[:, t, :], lhsT=wq[0][:, rows].bitcast(FP8X4), lhsT_scale=wq_sc[0][:, rows],
                                    rhs=eq[g][:, cols].bitcast(FP8X4), rhs_scale=eq_sc[g][:, cols], start=True, stop=True)

        def left_s(g, t):
            bank = psum.tile([P, GROUP], F32, name="bank_s", tag="bank_s")
            banks_s[g, t] = bank
            rows = slice(t * P, (t + 1) * P)
            nc.tensor.matmul_mx(out=bank[:], lhsT=wq[1][:, rows].bitcast(FP8X4), lhsT_scale=wq_sc[1][:, rows],
                                rhs=eq[g][:].bitcast(FP8X4), rhs_scale=eq_sc[g][:], start=True, stop=True)

        def exit_v(g, j):
            if j == 0:
                grouped = work.tile([P, GROUP, PACK], BF16, name="hg", tag="hg", align_bytes=64)
                hg[g] = grouped
            nc.vector.tensor_tensor(out=hg[g][:, j * P : (j + 1) * P, :], in0=banks_v[g, j][:].rearrange("p t n -> p n t"),
                                    in1=v_sb[:, 0, :].unsqueeze(1).to_broadcast([P, P, PACK]), op=ADD)

        def exit_s(g, t):
            if t == 0:
                planes_tile = work.tile([P, PACK, GROUP], BF16, name="planes", tag="planes", align_bytes=64)
                planes[g] = planes_tile
            nc.scalar.activation(out=planes[g][:, t, :], in_=banks_s[g, t][:], func=ACT.Identity, bias=v_sb[:, 1, t : t + 1])

        def weave(g, h):
            if h == 1 and g % 2 == 1:
                return
            bank = single.tile([P, HALF, PACK], BF16, name="woven", tag="flex")
            woven[g, h] = bank
            for j in range(2):
                cols = slice((2 * h + j) * P, (2 * h + j + 1) * P)
                nc.tensor.matmul(out=bank[:, j * P : (j + 1) * P, :].rearrange("p n t -> p t n"), lhsT=ident_bf[:],
                                 rhs=planes[g][:, :, cols], start=True, stop=True)

        def weave_exit(g, h):
            if h == 0:
                grouped = work.tile([P, GROUP, PACK], BF16, name="hi", tag="hi", align_bytes=64)
                hi[g] = grouped
            cols = slice(h * HALF, (h + 1) * HALF)
            if (g, h) in woven:
                nc.scalar.copy(out=hi[g][:, cols, :], in_=woven[g, h][:])
            else:
                nc.scalar.copy(out=hi[g][:, cols, :].rearrange("p (c i) t -> p c t i", i=4),
                               in_=planes[g][:, :, cols].rearrange("p t (c i) -> p c t i", i=4))

        def quantize_h(g, s):
            codes = work.tile([P, GROUP], U32, name=f"hq{s}", tag=f"hq{s}", align_bytes=64)
            sc = work.tile([P, GROUP], U8, name=f"hq_sc{s}", tag=f"hq_sc{s}", align_bytes=64)
            hq[g, s], hq_sc[g, s] = codes, sc
            src = (hg, hi)[s][g]
            nc.vector.quantize_mx(out=codes[:].bitcast(FP8X4), scales=sc[:], in_=src[:].rearrange("p n j -> p (n j)"))

        def right(g, s, h):
            bank = psum.tile([P, 2, N2], F32, name="sbank", tag="sbank")
            sbank[g, s, h] = bank
            for j in range(2):
                cols = slice((2 * h + j) * P, (2 * h + j + 1) * P)
                nc.tensor.matmul_mx(out=bank[:, j, :], lhsT=hq[g, s][:, cols].bitcast(FP8X4), lhsT_scale=hq_sc[g, s][:, cols],
                                    rhs=e2q[:].bitcast(FP8X4), rhs_scale=e2q_sc[:], start=True, stop=True)

        def tanh(g, s, h):
            z_tile = work.tile([P, 2 * N2], F32, name=f"z{s}{h}", tag=f"z{s}{h}", align_bytes=64)
            z[g, s, h] = z_tile
            nc.scalar.activation(out=z_tile[:], in_=sbank[g, s, h][:].rearrange("p j n -> p (j n)"), func=ACT.Tanh,
                                 bias=b_sb[:, s : s + 1], scale=D ** -0.5)

        def weigh(g, h):
            zw_tile = const.tile([P, 2 * N2], F32, name=f"zw{h}", tag=f"zw{h}", align_bytes=64)
            zw[g, h] = zw_tile
            nc.gpsimd.tensor_scalar(out=zw_tile[:], in0=z[g, 0, h][:], scalar1=u_f32[:, 0:1], scalar2=0.0, op0=MULT, op1=ADD)

        def combine(g, h):
            o = work.tile([P, 2 * N2], F32, name=f"o{h}", tag=f"o{h}", align_bytes=64)
            nc.vector.scalar_tensor_tensor(out=o[:], in0=z[g, 1, h][:], scalar=u_f32[:, 1:2], in1=zw[g, h][:], op0=MULT, op1=ADD)
            nc.sync.dma_start(out=out_rows[g][:, 2 * h : 2 * h + 2, :], in_=o[:].rearrange("p (j n) -> p j n", n=N2))

        def run(f, g, *args):
            if 0 <= g < GROUPS:
                f(g, *args)

        for i in range(-3, GROUPS + 3):
            run(weigh, i - 2, 1)
            if i == -1:
                e2_turn()
            if i == -3:
                spread_scale()
            if i == 1:
                e2_quantize()
            run(word_exit, i + 1, 1)
            run(quantize_e, i + 1)
            run(left_v, i, 0)
            run(tanh, i - 2, 0, 0)
            run(left_s, i, 1)
            run(exit_s, i, 2)
            run(weave, i - 1, 1)
            run(combine, i - 3, 0)
            run(tanh, i - 2, 1, 1)
            run(left_v, i, 1)
            run(exit_s, i, 1)
            if i == -2:
                w_interleave(0, nc.vector.tensor_copy)
            run(quantize_h, i - 1, 0)
            run(turn, i + 2, 0)
            if i == -1:
                e2_exit()
            run(weave_exit, i - 1, 1)
            run(exit_v, i, 0)
            run(right, i - 2, 1, 0)
            run(left_s, i + 1, 0)
            if i == -2:
                w_interleave(1, nc.scalar.copy)
            run(left_s, i + 1, 3)
            run(exit_v, i, 1)
            run(word_exit, i + 2, 0)
            run(prod, i + 3, 1)
            if i == -1:
                w_quantize(0)
            run(right, i - 1, 0, 1)
            run(tanh, i - 2, 1, 0)
            run(exit_s, i + 1, 0)
            run(combine, i - 2, 1)
            run(left_v, i, 3)
            run(tanh, i - 1, 0, 1)
            run(exit_s, i + 1, 3)
            run(weave, i, 0)
            run(weave_exit, i, 0)
            run(turn, i + 2, 1)
            run(quantize_h, i - 1, 1)
            run(right, i - 1, 0, 0)
            run(left_v, i, 2)
            run(exit_v, i, 3)
            if i == 0:
                nc.gpsimd.tensor_copy(out=u_f32[:], in_=u_sb[:])
            run(prod, i + 3, 0)
            run(left_s, i + 1, 2)
            run(weigh, i - 2, 0)
            if i == -2:
                w_quantize(1)
            run(exit_v, i, 2)
            run(right, i - 1, 1, 1)
